import numpy as np
CORES = [40,41,42,43,44,45,46,47,208,209,210,211,212,213,214,215]
N = 16
PERM = [[0,15],[1,14],[2,13],[3,12],[4,11],[5,10],[6,9],[7,8],[8,7],[9,6],[10,5],[11,4],[12,3],[13,2],[14,1],[15,0]]
def setup_inputs(rng):
    return {"x": rng.standard_normal((N, 128, 2048), dtype=np.float32)}
def reference(x):
    y = np.empty_like(x)
    for s, d in PERM:
        y[d] = x[s]
    return {"y": y}

@@ -1,0 +1,59 @@
+import comms_topo
+
+COLS = 2048
+PIECES = [16] * 8
+K = len(PIECES)
+ENG = 8
+
+SCRATCH = {}
+for _k in range(K):
+    SCRATCH["st%d" % _k] = ("dram", [128, PIECES[_k] * COLS // 128], "float32")
+    SCRATCH["ld%d" % _k] = ("dram", [128, PIECES[_k] * COLS // 128], "float32")
+SEMAPHORES = ["in%d" % _k for _k in range(K)] + ["ar%d" % _k for _k in range(K)] + ["sent", "stored"]
+
+
+def _plan(T, topo):
+    flows, used = [], set()
+    for s, d in T.tables["PERM"]:
+        src, dst = T.cores[s], T.cores[d]
+        if topo.may_write(src, dst):
+            flows.append((src, None, dst))
+            continue
+        base = topo.host(dst) * 128 + (topo.chip(dst) ^ 1) * 8
+        cand = [c for c in range(base, base + 8) if topo.may_write(c, dst) and c not in used]
+        same = [c for c in cand if topo.die(c) == topo.die(dst)]
+        h = (same or cand)[0]
+        used.add(h)
+        flows.append((src, h, dst))
+    return flows
+
+
+def _send(g, T, topo, core, to, k, buf):
+    rid, pid = topo.addr(to, core)
+    g.remote_dma(T["ld%d" % k][:], T[buf % k][:], T.sem["ar%d" % k], T.sem.sent, pid, rid, 0xFF)
+
+
+def rank_program(g, core, T, topo):
+    flows = _plan(T, topo)
+    lo = [sum(PIECES[:k]) for k in range(K + 1)]
+    nsent = 0
+    for src, via, dst in flows:
+        if core == src:
+            for k in range(K):
+                g.sync.dma_start(T["st%d" % k][:], T.x[lo[k]:lo[k + 1], :]).then_inc(T.sem["in%d" % k], 16)
+            for k in range(K):
+                g.wait_ge(T.sem["in%d" % k], 16)
+                _send(g, T, topo, core, dst if via is None else via, k, "st%d")
+                nsent += ENG
+        if core == via:
+            for k in range(K):
+                g.wait_ge(T.sem["ar%d" % k], ENG)
+                _send(g, T, topo, core, dst, k, "ld%d")
+                nsent += ENG
+        if core == dst:
+            for k in range(K):
+                g.scalar.wait_ge(T.sem["ar%d" % k], ENG)
+                g.scalar.dma_start(T.y[lo[k]:lo[k + 1], :], T["ld%d" % k][:]).then_inc(T.sem.stored, 16)
+            g.scalar.wait_ge(T.sem.stored, 16 * K)
+    if nsent:
+        g.wait_ge(T.sem.sent, nsent)

@@ -1,7 +1,7 @@
 import comms_topo
 
 COLS = 2048
-PIECES = [16] * 8
+PIECES = [8] * 16
 K = len(PIECES)
 ENG = 8
 

@@ -1,7 +1,7 @@
 import comms_topo
 
 COLS = 2048
-PIECES = [8] * 16
+PIECES = [4] * 32
 K = len(PIECES)
 ENG = 8
 

@@ -4,6 +4,7 @@ COLS = 2048
 PIECES = [4] * 32
 K = len(PIECES)
 ENG = 8
+DEPTH = 6
 
 SCRATCH = {}
 for _k in range(K):
@@ -40,6 +41,8 @@ def rank_program(g, core, T, topo):
     for src, via, dst in flows:
         if core == src:
             for k in range(K):
+                if k >= DEPTH:
+                    g.sync.wait_ge(T.sem["in%d" % (k - DEPTH)], 16)
                 g.sync.dma_start(T["st%d" % k][:], T.x[lo[k]:lo[k + 1], :]).then_inc(T.sem["in%d" % k], 16)
             for k in range(K):
                 g.wait_ge(T.sem["in%d" % k], 16)

import comms_topo

COLS = 2048
PIECES = [4] * 32
K = len(PIECES)
ENG = 8
DEPTH = 6

SCRATCH = {}
for _k in range(K):
    SCRATCH["st%d" % _k] = ("dram", [128, PIECES[_k] * COLS // 128], "float32")
    SCRATCH["ld%d" % _k] = ("dram", [128, PIECES[_k] * COLS // 128], "float32")
SEMAPHORES = ["in%d" % _k for _k in range(K)] + ["ar%d" % _k for _k in range(K)] + ["sent", "stored"]


def _plan(T, topo):
    flows, used = [], set()
    for s, d in T.tables["PERM"]:
        src, dst = T.cores[s], T.cores[d]
        if topo.may_write(src, dst):
            flows.append((src, None, dst))
            continue
        base = topo.host(dst) * 128 + (topo.chip(dst) ^ 1) * 8
        cand = [c for c in range(base, base + 8) if topo.may_write(c, dst) and c not in used]
        same = [c for c in cand if topo.die(c) == topo.die(dst)]
        h = (same or cand)[0]
        used.add(h)
        flows.append((src, h, dst))
    return flows


def _send(g, T, topo, core, to, k, buf):
    rid, pid = topo.addr(to, core)
    g.remote_dma(T["ld%d" % k][:], T[buf % k][:], T.sem["ar%d" % k], T.sem.sent, pid, rid, 0xFF)


def rank_program(g, core, T, topo):
    flows = _plan(T, topo)
    lo = [sum(PIECES[:k]) for k in range(K + 1)]
    nsent = 0
    for src, via, dst in flows:
        if core == src:
            for k in range(K):
                if k >= DEPTH:
                    g.sync.wait_ge(T.sem["in%d" % (k - DEPTH)], 16)
                g.sync.dma_start(T["st%d" % k][:], T.x[lo[k]:lo[k + 1], :]).then_inc(T.sem["in%d" % k], 16)
            for k in range(K):
                g.wait_ge(T.sem["in%d" % k], 16)
                _send(g, T, topo, core, dst if via is None else via, k, "st%d")
                nsent += ENG
        if core == via:
            for k in range(K):
                g.wait_ge(T.sem["ar%d" % k], ENG)
                _send(g, T, topo, core, dst, k, "ld%d")
                nsent += ENG
        if core == dst:
            for k in range(K):
                g.scalar.wait_ge(T.sem["ar%d" % k], ENG)
                g.scalar.dma_start(T.y[lo[k]:lo[k + 1], :], T["ld%d" % k][:]).then_inc(T.sem.stored, 16)
            g.scalar.wait_ge(T.sem.stored, 16 * K)
    if nsent:
        g.wait_ge(T.sem.sent, nsent)
